import numpy as np
import ml_dtypes


def mxq(x, axis, fmt="e4m3"):
    dtype, down = {"e4m3": (ml_dtypes.float8_e4m3fn, 7), "e5m2": (ml_dtypes.float8_e5m2, 14)}[fmt]
    v = np.moveaxis(np.asarray(x, np.float32).astype(ml_dtypes.bfloat16).astype(np.float64), axis, -1)
    blocks = v.reshape(v.shape[:-1] + (-1, 32))
    amax = np.abs(blocks).max(-1, keepdims=True)
    byte = np.maximum(np.where(amax > 0, np.frexp(amax)[1] - 1 + 127, 0) - down, 1)
    scale = np.exp2(byte - 127.0)
    codes = (blocks / scale).astype(np.float32).astype(dtype).astype(np.float64)
    return np.moveaxis((codes * scale).reshape(v.shape), -1, axis)


WIDE = False


def mx_kscale(k):
    if not WIDE:
        return np.ones(k)
    levels = np.array([10, -10, 5, -5, 0])
    if k % 512:
        return np.exp2(np.random.permutation(np.resize(levels, k // 32))).repeat(32)
    a = np.empty((k // 512, 16))
    for p in range(k // 512):
        a[p, :8] = np.random.permutation(np.resize(levels, 8))
        for g in range(8):
            far = levels[np.abs(levels - a[p, g]) >= 10]
            a[p, g + 8] = far[np.random.randint(len(far))]
    return np.exp2(a.ravel()).repeat(32)


def f64(x):
    return np.asarray(x).astype(np.float64)


def striped8(idx):
    return np.concatenate([x.reshape(-1, 16).T for x in idx]).astype(np.uint16)


def runs(offs, k):
    lists = np.stack([offs[16 * r : 16 * r + 16].T.reshape(-1) for r in range(8)]).astype(np.int64)
    return lists[np.arange(k) % 512 // 64]


def pack_weight(w):
    k, n = w.shape
    w = f64(np.asarray(w, np.float32).astype(ml_dtypes.bfloat16)).reshape(k // 32, 32, n)
    amax = np.abs(w).max(1)
    byte = np.clip(np.where(amax > 0, np.frexp(amax)[1] - 1 + 127 - 7, 1), 1, 254)
    scaled = (w * np.exp2(127.0 - byte)[:, None, :]).reshape(k, n).astype(np.float32)
    words = np.ascontiguousarray(scaled.reshape(k // 512, 128, 4, n).transpose(0, 1, 3, 2)).astype(ml_dtypes.float8_e4m3fn).view(np.uint8)
    return words, np.ascontiguousarray(byte.astype(np.uint8).reshape(k // 512, 16, n))


def unpack_weight(words, scales):
    g, p, n, _ = words.shape
    vals = np.ascontiguousarray(words).view(ml_dtypes.float8_e4m3fn).astype(np.float64) * np.repeat(np.exp2(scales.astype(np.float64) - 127.0), 8, axis=1)[..., None]
    return vals.transpose(0, 1, 3, 2).reshape(g * 512, n)


def relu(v):
    return np.maximum(v, 0.0)


K, T, S, H, N = 512, 2048, 1024, 512, 256


def setup_inputs():
    n = np.random.standard_normal
    s = mx_kscale(K)[:, None]
    u = mx_kscale(H)
    packed_xT = pack_weight(n((K, T)) * s)
    return {
        "x_words": packed_xT[0],
        "x_scales": packed_xT[1],
        "w1": (n((K, H)) / np.sqrt(K) / s * u).astype(np.float32),
        "w2": (n((H, N)) / np.sqrt(H) / u[:, None]).astype(np.float32),
        "offs": striped8(np.stack([np.random.permutation(T)[:S] for _ in range(8)])),
    }


def reference(x_words, x_scales, w1, w2, offs):
    xq = unpack_weight(x_words, x_scales)[np.arange(K)[:, None], runs(offs, K)]
    h = relu(mxq(f64(w1), 0, "e4m3").T @ xq)
    return mxq(f64(w2), 0, "e4m3").T @ mxq(h, 0, "e4m3")

@@ -1,0 +1,152 @@
+from contextlib import ExitStack
+
+import concourse.mybir as mybir
+
+K, T, S, H, N = 512, 2048, 1024, 512, 256
+FLOPS = 2 * K * H * S + 2 * H * N * S
+
+F32 = mybir.dt.float32
+BF16 = mybir.dt.bfloat16
+I32 = mybir.dt.int32
+U32 = mybir.dt.uint32
+U16 = mybir.dt.uint16
+U8 = mybir.dt.uint8
+FP8X4 = mybir.dt.float8_e4m3fn_x4
+RELU = mybir.ActivationFunctionType.Relu
+COPY = mybir.ActivationFunctionType.Copy
+
+P = 128
+PACK = 4
+PIECE = 256
+CHUNK = 128
+W1_SCALAR = 64
+
+
+def tile_picked_phmlp_relu_p_kernel(tc, x_words, x_scales, w1, w2, offs, out):
+    nc = tc.nc
+    pieces = S // PIECE
+    with ExitStack() as ctx:
+        keep = ctx.enter_context(tc.tile_pool(name="keep", bufs=1))
+        hpsum = ctx.enter_context(tc.psum_pool(name="hpsum", bufs=6))
+        opsum = ctx.enter_context(tc.psum_pool(name="opsum", bufs=2))
+
+        offsets = keep.tile([P, S // 16], U16, name="offsets")
+        nc.sync.dma_start(offsets[:], offs)
+
+        scale_table = keep.tile([P, T], U8, name="scale_table", align_bytes=64)
+        nc.vector.memset(scale_table[:].bitcast(I32), 0)
+        nc.scalar.dma_start(out=scale_table[0:P:8, :].bitcast(I32), in_=x_scales[0].bitcast(I32))
+        x_plane = keep.tile([P, S], U8, name="x_plane", align_bytes=64)
+        nc.vector.memset(x_plane[:].bitcast(I32), 0)
+
+        w1_raw = keep.tile([P, PACK, H], F32, name="w1_raw", tag="w_raw")
+        nc.sync.dma_start(out=w1_raw[:], in_=w1.rearrange("(p j) c -> p j c", j=PACK))
+        word_table = keep.tile([P, T], U32, name="word_table", align_bytes=64)
+        nc.sync.dma_start(
+            out=word_table[:].bitcast(I32), in_=x_words[0].rearrange("p c r -> p (c r)").bitcast(I32)
+        )
+
+        picked_scales = keep.tile([P, S], U8, name="picked_scales", align_bytes=64)
+        nc.vector.tensor_copy(picked_scales[:], scale_table[:].indirect(offsets[:]))
+        for b in range(4):
+            nc.sync.dma_start(
+                out=x_plane[b:P:32, :].bitcast(I32), in_=picked_scales[8 * b : P : 32, :].bitcast(I32)
+            )
+
+        w1_bf = keep.tile([P, PACK * P * PACK], BF16, name="w1_bf", align_bytes=64)
+        dst = w1_bf[:].rearrange("p (t m j) -> p m t j", t=PACK, j=PACK)
+        src = w1_raw[:].rearrange("p j (m t) -> p m t j", t=PACK)
+        nc.scalar.activation(dst[:, :W1_SCALAR], src[:, :W1_SCALAR], COPY)
+        nc.vector.tensor_copy(dst[:, W1_SCALAR:], src[:, W1_SCALAR:])
+        w1_codes = keep.tile([P, H], U32, name="w1_codes", align_bytes=64)
+        w1_plane = keep.tile([P, H], U8, name="w1_plane", align_bytes=64)
+        nc.vector.quantize_mx(out=w1_codes[:].bitcast(FP8X4), scales=w1_plane[:], in_=w1_bf[:])
+
+        w2_raw = keep.tile([P, PACK, N], F32, name="w2_raw", tag="w_raw")
+        nc.sync.dma_start(out=w2_raw[:], in_=w2.rearrange("(p j) n -> p j n", j=PACK))
+
+        picked = []
+        for g in range(pieces):
+            words = keep.tile([P, PIECE], U32, name="picked_words%d" % g, align_bytes=64)
+            lists = offsets[:, g * PIECE // 16 : (g + 1) * PIECE // 16]
+            nc.vector.tensor_copy(words[:], word_table[:].indirect(lists))
+            picked.append(words)
+
+        w2_bf = keep.tile([P, N * PACK], BF16, name="w2_bf", align_bytes=64)
+        nc.vector.tensor_copy(
+            w2_bf[:].rearrange("p (c i j) -> p c j i", i=4, j=PACK),
+            w2_raw[:].rearrange("p j (c i) -> p c j i", i=4),
+        )
+        w2_codes = keep.tile([P, N], U32, name="w2_codes", align_bytes=64)
+        w2_plane = keep.tile([P, N], U8, name="w2_plane", align_bytes=64)
+
+        def first_layer(c):
+            g, half = divmod(c, PIECE // CHUNK)
+            bank = hpsum.tile([P, PACK, CHUNK], F32, name="h_bank")
+            for t in range(PACK):
+                nc.tensor.matmul_mx(
+                    out=bank[:, t, :],
+                    lhsT=w1_codes[:, t * P : (t + 1) * P].bitcast(FP8X4),
+                    lhsT_scale=w1_plane[:, t * P : (t + 1) * P],
+                    rhs=picked[g][:, half * CHUNK : (half + 1) * CHUNK].bitcast(FP8X4),
+                    rhs_scale=x_plane[:, c * CHUNK : (c + 1) * CHUNK],
+                    start=True,
+                    stop=True,
+                )
+            return bank
+
+        h_bf = [keep.tile([P, PIECE * PACK], BF16, name="h_bf%d" % g, align_bytes=64) for g in range(pieces)]
+        h_codes = [keep.tile([P, PIECE], U32, name="h_codes%d" % g, align_bytes=64) for g in range(pieces)]
+        h_plane = [keep.tile([P, PIECE], U8, name="h_plane%d" % g, align_bytes=64) for g in range(pieces)]
+
+        def hidden(c, on_vector):
+            g, half = divmod(c, PIECE // CHUNK)
+            bank = first_layer(c)
+            dst_h = h_bf[g][:, half * CHUNK * PACK : (half + 1) * CHUNK * PACK].rearrange("p (n t) -> p n t", t=PACK)
+            src_h = bank[:].rearrange("p t n -> p n t")
+            if on_vector:
+                nc.vector.tensor_scalar_max(dst_h, src_h, 0.0)
+            else:
+                nc.scalar.activation(dst_h, src_h, RELU)
+
+        def quantize_hidden(g):
+            nc.vector.quantize_mx(out=h_codes[g][:].bitcast(FP8X4), scales=h_plane[g][:], in_=h_bf[g][:])
+
+        out_view = out.rearrange("(u p) n -> p u n", p=P)
+
+        def second_layer(g, on_vector):
+            bank = opsum.tile([P, N // P, PIECE], F32, name="o_bank")
+            for u in range(N // P):
+                nc.tensor.matmul_mx(
+                    out=bank[:, u, :],
+                    lhsT=w2_codes[:, u * P : (u + 1) * P].bitcast(FP8X4),
+                    lhsT_scale=w2_plane[:, u * P : (u + 1) * P],
+                    rhs=h_codes[g][:].bitcast(FP8X4),
+                    rhs_scale=h_plane[g][:],
+                    start=True,
+                    stop=True,
+                )
+            staged = keep.tile([P, N // P, PIECE], F32, name="staged%d" % g)
+            if on_vector:
+                nc.vector.tensor_copy(staged[:], bank[:])
+            else:
+                nc.scalar.copy(staged[:], bank[:])
+            nc.sync.dma_start(out=out_view[:, :, g * PIECE : (g + 1) * PIECE], in_=staged[:])
+
+        hidden(0, False)
+        hidden(1, False)
+        nc.vector.quantize_mx(out=w2_codes[:].bitcast(FP8X4), scales=w2_plane[:], in_=w2_bf[:])
+        hidden(2, False)
+        quantize_hidden(0)
+        hidden(3, False)
+        hidden(4, False)
+        hidden(5, True)
+        quantize_hidden(1)
+        second_layer(0, False)
+        hidden(6, False)
+        hidden(7, True)
+        quantize_hidden(2)
+        second_layer(1, False)
+        quantize_hidden(3)
+        second_layer(2, False)
+        second_layer(3, True)

@@ -19,7 +19,7 @@ P = 128
 PACK = 4
 PIECE = 256
 CHUNK = 128
-W1_SCALAR = 64
+HEAD = 768
 
 
 def tile_picked_phmlp_relu_p_kernel(tc, x_words, x_scales, w1, w2, offs, out):
@@ -27,24 +27,30 @@ def tile_picked_phmlp_relu_p_kernel(tc, x_words, x_scales, w1, w2, offs, out):
     pieces = S // PIECE
     with ExitStack() as ctx:
         keep = ctx.enter_context(tc.tile_pool(name="keep", bufs=1))
-        hpsum = ctx.enter_context(tc.psum_pool(name="hpsum", bufs=6))
-        opsum = ctx.enter_context(tc.psum_pool(name="opsum", bufs=2))
+        psum = ctx.enter_context(tc.psum_pool(name="psum", bufs=8))
 
+        word_table = keep.tile([P, T], U32, name="word_table", align_bytes=64)
+        word_rows = x_words[0].rearrange("p c r -> p (c r)").bitcast(I32)
+        nc.sync.dma_start(out=word_table[:, :HEAD].bitcast(I32), in_=word_rows[:, :HEAD])
         offsets = keep.tile([P, S // 16], U16, name="offsets")
         nc.sync.dma_start(offsets[:], offs)
 
         scale_table = keep.tile([P, T], U8, name="scale_table", align_bytes=64)
         nc.vector.memset(scale_table[:].bitcast(I32), 0)
-        nc.scalar.dma_start(out=scale_table[0:P:8, :].bitcast(I32), in_=x_scales[0].bitcast(I32))
+        nc.sync.dma_start(out=scale_table[0:P:8, :].bitcast(I32), in_=x_scales[0].bitcast(I32))
         x_plane = keep.tile([P, S], U8, name="x_plane", align_bytes=64)
         nc.vector.memset(x_plane[:].bitcast(I32), 0)
 
-        w1_raw = keep.tile([P, PACK, H], F32, name="w1_raw", tag="w_raw")
-        nc.sync.dma_start(out=w1_raw[:], in_=w1.rearrange("(p j) c -> p j c", j=PACK))
-        word_table = keep.tile([P, T], U32, name="word_table", align_bytes=64)
-        nc.sync.dma_start(
-            out=word_table[:].bitcast(I32), in_=x_words[0].rearrange("p c r -> p (c r)").bitcast(I32)
-        )
+        nc.sync.dma_start(out=word_table[:, HEAD:].bitcast(I32), in_=word_rows[:, HEAD:])
+        w1_rows = w1.rearrange("(p j) c -> p j c", j=PACK)
+        w1_raw = []
+        for half in range(2):
+            raw = keep.tile([P, PACK, H // 2], F32, name="w1_raw%d" % half)
+            nc.sync.dma_start(out=raw[:], in_=w1_rows[:, :, half * H // 2 : (half + 1) * H // 2])
+            w1_raw.append(raw)
+
+        w2_raw = keep.tile([P, PACK, N], F32, name="w2_raw")
+        nc.sync.dma_start(out=w2_raw[:], in_=w2.rearrange("(p j) n -> p j n", j=PACK))
 
         picked_scales = keep.tile([P, S], U8, name="picked_scales", align_bytes=64)
         nc.vector.tensor_copy(picked_scales[:], scale_table[:].indirect(offsets[:]))
@@ -53,36 +59,62 @@ def tile_picked_phmlp_relu_p_kernel(tc, x_words, x_scales, w1, w2, offs, out):
                 out=x_plane[b:P:32, :].bitcast(I32), in_=picked_scales[8 * b : P : 32, :].bitcast(I32)
             )
 
-        w1_bf = keep.tile([P, PACK * P * PACK], BF16, name="w1_bf", align_bytes=64)
-        dst = w1_bf[:].rearrange("p (t m j) -> p m t j", t=PACK, j=PACK)
-        src = w1_raw[:].rearrange("p j (m t) -> p m t j", t=PACK)
-        nc.scalar.activation(dst[:, :W1_SCALAR], src[:, :W1_SCALAR], COPY)
-        nc.vector.tensor_copy(dst[:, W1_SCALAR:], src[:, W1_SCALAR:])
-        w1_codes = keep.tile([P, H], U32, name="w1_codes", align_bytes=64)
-        w1_plane = keep.tile([P, H], U8, name="w1_plane", align_bytes=64)
-        nc.vector.quantize_mx(out=w1_codes[:].bitcast(FP8X4), scales=w1_plane[:], in_=w1_bf[:])
-
-        w2_raw = keep.tile([P, PACK, N], F32, name="w2_raw", tag="w_raw")
-        nc.sync.dma_start(out=w2_raw[:], in_=w2.rearrange("(p j) n -> p j n", j=PACK))
-
         picked = []
-        for g in range(pieces):
-            words = keep.tile([P, PIECE], U32, name="picked_words%d" % g, align_bytes=64)
+
+        def gather_words(g, tag):
+            words = keep.tile([P, PIECE], U32, name="picked_words%d" % g, tag=tag, align_bytes=64)
             lists = offsets[:, g * PIECE // 16 : (g + 1) * PIECE // 16]
             nc.vector.tensor_copy(words[:], word_table[:].indirect(lists))
             picked.append(words)
 
+        for g in range(pieces - 1):
+            gather_words(g, "picked_words%d" % g)
+
+        warm_bank = psum.tile([P, PIECE], F32, name="warm_bank", tag="bank")
+        for turn in range(6):
+            nc.tensor.matmul_mx(
+                out=warm_bank[:],
+                lhsT=picked[0][:, :P].bitcast(FP8X4),
+                lhsT_scale=picked_scales[:, :P],
+                rhs=picked[0][:].bitcast(FP8X4),
+                rhs_scale=picked_scales[:, :PIECE],
+                start=True,
+                stop=True,
+            )
+
+        w1_bf = keep.tile([P, PACK * P * PACK], BF16, name="w1_bf", tag="w1_bf_then_words", align_bytes=64)
+        dst = w1_bf[:].rearrange("p (t m j) -> p m t j", t=PACK, j=PACK)
+        src = [raw[:].rearrange("p j (m t) -> p m t j", t=PACK) for raw in w1_raw]
+        mid = P // 2
+        nc.scalar.activation(dst[:, :mid], src[0], COPY)
+        nc.scalar.activation(dst[:, mid:], src[1], COPY)
+        w1_codes = keep.tile([P, H], U32, name="w1_codes", align_bytes=64)
+        w1_plane = keep.tile([P, H], U8, name="w1_plane", align_bytes=64)
+        for half in range(2):
+            cols = slice(half * H // 2, (half + 1) * H // 2)
+            nc.vector.quantize_mx(
+                out=w1_codes[:, cols].bitcast(FP8X4),
+                scales=w1_plane[:, cols],
+                in_=w1_bf[:, half * H * PACK // 2 : (half + 1) * H * PACK // 2],
+            )
+        gather_words(pieces - 1, "w1_bf_then_words")
+
         w2_bf = keep.tile([P, N * PACK], BF16, name="w2_bf", align_bytes=64)
-        nc.vector.tensor_copy(
+        nc.scalar.activation(
             w2_bf[:].rearrange("p (c i j) -> p c j i", i=4, j=PACK),
             w2_raw[:].rearrange("p j (c i) -> p c j i", i=4),
+            COPY,
         )
         w2_codes = keep.tile([P, N], U32, name="w2_codes", align_bytes=64)
         w2_plane = keep.tile([P, N], U8, name="w2_plane", align_bytes=64)
 
-        def first_layer(c):
+        h_bf = [keep.tile([P, PIECE * PACK], BF16, name="h_bf%d" % g, align_bytes=64) for g in range(pieces)]
+        h_codes = [keep.tile([P, PIECE], U32, name="h_codes%d" % g, align_bytes=64) for g in range(pieces)]
+        h_plane = [keep.tile([P, PIECE], U8, name="h_plane%d" % g, align_bytes=64) for g in range(pieces)]
+
+        def hidden(c, on_vector):
             g, half = divmod(c, PIECE // CHUNK)
-            bank = hpsum.tile([P, PACK, CHUNK], F32, name="h_bank")
+            bank = psum.tile([P, PACK, CHUNK], F32, name="h_bank", tag="bank")
             for t in range(PACK):
                 nc.tensor.matmul_mx(
                     out=bank[:, t, :],
@@ -93,15 +125,6 @@ def tile_picked_phmlp_relu_p_kernel(tc, x_words, x_scales, w1, w2, offs, out):
                     start=True,
                     stop=True,
                 )
-            return bank
-
-        h_bf = [keep.tile([P, PIECE * PACK], BF16, name="h_bf%d" % g, align_bytes=64) for g in range(pieces)]
-        h_codes = [keep.tile([P, PIECE], U32, name="h_codes%d" % g, align_bytes=64) for g in range(pieces)]
-        h_plane = [keep.tile([P, PIECE], U8, name="h_plane%d" % g, align_bytes=64) for g in range(pieces)]
-
-        def hidden(c, on_vector):
-            g, half = divmod(c, PIECE // CHUNK)
-            bank = first_layer(c)
             dst_h = h_bf[g][:, half * CHUNK * PACK : (half + 1) * CHUNK * PACK].rearrange("p (n t) -> p n t", t=PACK)
             src_h = bank[:].rearrange("p t n -> p n t")
             if on_vector:
@@ -114,11 +137,11 @@ def tile_picked_phmlp_relu_p_kernel(tc, x_words, x_scales, w1, w2, offs, out):
 
         out_view = out.rearrange("(u p) n -> p u n", p=P)
 
-        def second_layer(g, on_vector):
-            bank = opsum.tile([P, N // P, PIECE], F32, name="o_bank")
-            for u in range(N // P):
+        def second_layer(g, rows, on_vector):
+            bank = psum.tile([P, len(rows), PIECE], F32, name="o_bank", tag="bank")
+            for slot, u in enumerate(rows):
                 nc.tensor.matmul_mx(
-                    out=bank[:, u, :],
+                    out=bank[:, slot, :],
                     lhsT=w2_codes[:, u * P : (u + 1) * P].bitcast(FP8X4),
                     lhsT_scale=w2_plane[:, u * P : (u + 1) * P],
                     rhs=h_codes[g][:].bitcast(FP8X4),
@@ -126,27 +149,30 @@ def tile_picked_phmlp_relu_p_kernel(tc, x_words, x_scales, w1, w2, offs, out):
                     start=True,
                     stop=True,
                 )
-            staged = keep.tile([P, N // P, PIECE], F32, name="staged%d" % g)
+            staged = keep.tile([P, len(rows), PIECE], F32, name="staged%d_%d" % (g, rows[0]))
             if on_vector:
                 nc.vector.tensor_copy(staged[:], bank[:])
             else:
                 nc.scalar.copy(staged[:], bank[:])
-            nc.sync.dma_start(out=out_view[:, :, g * PIECE : (g + 1) * PIECE], in_=staged[:])
+            nc.sync.dma_start(
+                out=out_view[:, rows[0] : rows[-1] + 1, g * PIECE : (g + 1) * PIECE], in_=staged[:]
+            )
 
         hidden(0, False)
-        hidden(1, False)
         nc.vector.quantize_mx(out=w2_codes[:].bitcast(FP8X4), scales=w2_plane[:], in_=w2_bf[:])
-        hidden(2, False)
+        hidden(1, False)
+        hidden(2, True)
         quantize_hidden(0)
         hidden(3, False)
+        quantize_hidden(1)
         hidden(4, False)
         hidden(5, True)
-        quantize_hidden(1)
-        second_layer(0, False)
-        hidden(6, False)
-        hidden(7, True)
+        second_layer(0, [0, 1], False)
         quantize_hidden(2)
-        second_layer(1, False)
+        hidden(7, False)
+        hidden(6, True)
+        second_layer(1, [0, 1], False)
         quantize_hidden(3)
-        second_layer(2, False)
-        second_layer(3, True)
+        second_layer(2, [0, 1], False)
+        second_layer(3, [0], True)
+        second_layer(3, [1], False)

@@ -83,11 +83,13 @@ def tile_picked_phmlp_relu_p_kernel(tc, x_words, x_scales, w1, w2, offs, out):
             )
 
         w1_bf = keep.tile([P, PACK * P * PACK], BF16, name="w1_bf", tag="w1_bf_then_words", align_bytes=64)
-        dst = w1_bf[:].rearrange("p (t m j) -> p m t j", t=PACK, j=PACK)
-        src = [raw[:].rearrange("p j (m t) -> p m t j", t=PACK) for raw in w1_raw]
+        dst = w1_bf[:].rearrange("p (t m j) -> p m j t", t=PACK, j=PACK)
+        src = [raw[:].rearrange("p j (m t) -> p m j t", t=PACK) for raw in w1_raw]
         mid = P // 2
-        nc.scalar.activation(dst[:, :mid], src[0], COPY)
-        nc.scalar.activation(dst[:, mid:], src[1], COPY)
+        for half in range(2):
+            for pair in range(2):
+                tiles = slice(2 * pair, 2 * pair + 2)
+                nc.scalar.activation(dst[:, half * mid : (half + 1) * mid, :, tiles], src[half][:, :, :, tiles], COPY)
         w1_codes = keep.tile([P, H], U32, name="w1_codes", align_bytes=64)
         w1_plane = keep.tile([P, H], U8, name="w1_plane", align_bytes=64)
         for half in range(2):

@@ -41,13 +41,14 @@ def tile_picked_phmlp_relu_p_kernel(tc, x_words, x_scales, w1, w2, offs, out):
         x_plane = keep.tile([P, S], U8, name="x_plane", align_bytes=64)
         nc.vector.memset(x_plane[:].bitcast(I32), 0)
 
-        nc.sync.dma_start(out=word_table[:, HEAD:].bitcast(I32), in_=word_rows[:, HEAD:])
         w1_rows = w1.rearrange("(p j) c -> p j c", j=PACK)
         w1_raw = []
         for half in range(2):
             raw = keep.tile([P, PACK, H // 2], F32, name="w1_raw%d" % half)
             nc.sync.dma_start(out=raw[:], in_=w1_rows[:, :, half * H // 2 : (half + 1) * H // 2])
             w1_raw.append(raw)
+            if half == 0:
+                nc.sync.dma_start(out=word_table[:, HEAD:].bitcast(I32), in_=word_rows[:, HEAD:])
 
         w2_raw = keep.tile([P, PACK, N], F32, name="w2_raw")
         nc.sync.dma_start(out=w2_raw[:], in_=w2.rearrange("(p j) n -> p j n", j=PACK))
@@ -71,7 +72,7 @@ def tile_picked_phmlp_relu_p_kernel(tc, x_words, x_scales, w1, w2, offs, out):
             gather_words(g, "picked_words%d" % g)
 
         warm_bank = psum.tile([P, PIECE], F32, name="warm_bank", tag="bank")
-        for turn in range(6):
+        for turn in range(4):
             nc.tensor.matmul_mx(
                 out=warm_bank[:],
                 lhsT=picked[0][:, :P].bitcast(FP8X4),

@@ -44,8 +44,8 @@ def tile_picked_phmlp_relu_p_kernel(tc, x_words, x_scales, w1, w2, offs, out):
         w1_rows = w1.rearrange("(p j) c -> p j c", j=PACK)
         w1_raw = []
         for half in range(2):
-            raw = keep.tile([P, PACK, H // 2], F32, name="w1_raw%d" % half)
-            nc.sync.dma_start(out=raw[:], in_=w1_rows[:, :, half * H // 2 : (half + 1) * H // 2])
+            raw = keep.tile([P, PACK // 2, H], F32, name="w1_raw%d" % half)
+            nc.sync.dma_start(out=raw[:], in_=w1_rows[:, 2 * half : 2 * half + 2, :])
             w1_raw.append(raw)
             if half == 0:
                 nc.sync.dma_start(out=word_table[:, HEAD:].bitcast(I32), in_=word_rows[:, HEAD:])
@@ -86,11 +86,10 @@ def tile_picked_phmlp_relu_p_kernel(tc, x_words, x_scales, w1, w2, offs, out):
         w1_bf = keep.tile([P, PACK * P * PACK], BF16, name="w1_bf", tag="w1_bf_then_words", align_bytes=64)
         dst = w1_bf[:].rearrange("p (t m j) -> p m j t", t=PACK, j=PACK)
         src = [raw[:].rearrange("p j (m t) -> p m j t", t=PACK) for raw in w1_raw]
-        mid = P // 2
         for half in range(2):
             for pair in range(2):
                 tiles = slice(2 * pair, 2 * pair + 2)
-                nc.scalar.activation(dst[:, half * mid : (half + 1) * mid, :, tiles], src[half][:, :, :, tiles], COPY)
+                nc.scalar.activation(dst[:, :, 2 * half : 2 * half + 2, tiles], src[half][:, :, :, tiles], COPY)
         w1_codes = keep.tile([P, H], U32, name="w1_codes", align_bytes=64)
         w1_plane = keep.tile([P, H], U8, name="w1_plane", align_bytes=64)
         for half in range(2):

@@ -17,9 +17,15 @@ COPY = mybir.ActivationFunctionType.Copy
 
 P = 128
 PACK = 4
+LIST_ROWS = 16
+BLOCK_ROWS = 8
+QUADRANT = 32
+BANKS = 8
 PIECE = 256
 CHUNK = 128
 HEAD = 768
+SPLIT = 64
+WARM_PASSES = 4
 
 
 def tile_picked_phmlp_relu_p_kernel(tc, x_words, x_scales, w1, w2, offs, out):
@@ -27,27 +33,27 @@ def tile_picked_phmlp_relu_p_kernel(tc, x_words, x_scales, w1, w2, offs, out):
     pieces = S // PIECE
     with ExitStack() as ctx:
         keep = ctx.enter_context(tc.tile_pool(name="keep", bufs=1))
-        psum = ctx.enter_context(tc.psum_pool(name="psum", bufs=8))
+        psum = ctx.enter_context(tc.psum_pool(name="psum", bufs=BANKS))
 
         word_table = keep.tile([P, T], U32, name="word_table", align_bytes=64)
         word_rows = x_words[0].rearrange("p c r -> p (c r)").bitcast(I32)
         nc.sync.dma_start(out=word_table[:, :HEAD].bitcast(I32), in_=word_rows[:, :HEAD])
-        offsets = keep.tile([P, S // 16], U16, name="offsets")
+        offsets = keep.tile([P, S // LIST_ROWS], U16, name="offsets")
         nc.sync.dma_start(offsets[:], offs)
 
         scale_table = keep.tile([P, T], U8, name="scale_table", align_bytes=64)
         nc.vector.memset(scale_table[:].bitcast(I32), 0)
-        nc.sync.dma_start(out=scale_table[0:P:8, :].bitcast(I32), in_=x_scales[0].bitcast(I32))
+        nc.sync.dma_start(out=scale_table[0:P:BLOCK_ROWS, :].bitcast(I32), in_=x_scales[0].bitcast(I32))
         x_plane = keep.tile([P, S], U8, name="x_plane", align_bytes=64)
         nc.vector.memset(x_plane[:].bitcast(I32), 0)
 
         w1_rows = w1.rearrange("(p j) c -> p j c", j=PACK)
         w1_raw = []
-        for half in range(2):
-            raw = keep.tile([P, PACK // 2, H], F32, name="w1_raw%d" % half)
-            nc.sync.dma_start(out=raw[:], in_=w1_rows[:, 2 * half : 2 * half + 2, :])
+        for row_pair in range(2):
+            raw = keep.tile([P, PACK // 2, H], F32, name="w1_raw%d" % row_pair)
+            nc.sync.dma_start(out=raw[:], in_=w1_rows[:, 2 * row_pair : 2 * row_pair + 2, :])
             w1_raw.append(raw)
-            if half == 0:
+            if row_pair == 0:
                 nc.sync.dma_start(out=word_table[:, HEAD:].bitcast(I32), in_=word_rows[:, HEAD:])
 
         w2_raw = keep.tile([P, PACK, N], F32, name="w2_raw")
@@ -55,16 +61,17 @@ def tile_picked_phmlp_relu_p_kernel(tc, x_words, x_scales, w1, w2, offs, out):
 
         picked_scales = keep.tile([P, S], U8, name="picked_scales", align_bytes=64)
         nc.vector.tensor_copy(picked_scales[:], scale_table[:].indirect(offsets[:]))
-        for b in range(4):
+        for r in range(QUADRANT // BLOCK_ROWS):
             nc.sync.dma_start(
-                out=x_plane[b:P:32, :].bitcast(I32), in_=picked_scales[8 * b : P : 32, :].bitcast(I32)
+                out=x_plane[r:P:QUADRANT, :].bitcast(I32),
+                in_=picked_scales[BLOCK_ROWS * r : P : QUADRANT, :].bitcast(I32),
             )
 
         picked = []
 
         def gather_words(g, tag):
             words = keep.tile([P, PIECE], U32, name="picked_words%d" % g, tag=tag, align_bytes=64)
-            lists = offsets[:, g * PIECE // 16 : (g + 1) * PIECE // 16]
+            lists = offsets[:, g * PIECE // LIST_ROWS : (g + 1) * PIECE // LIST_ROWS]
             nc.vector.tensor_copy(words[:], word_table[:].indirect(lists))
             picked.append(words)
 
@@ -72,7 +79,7 @@ def tile_picked_phmlp_relu_p_kernel(tc, x_words, x_scales, w1, w2, offs, out):
             gather_words(g, "picked_words%d" % g)
 
         warm_bank = psum.tile([P, PIECE], F32, name="warm_bank", tag="bank")
-        for turn in range(4):
+        for turn in range(WARM_PASSES):
             nc.tensor.matmul_mx(
                 out=warm_bank[:],
                 lhsT=picked[0][:, :P].bitcast(FP8X4),
@@ -86,18 +93,20 @@ def tile_picked_phmlp_relu_p_kernel(tc, x_words, x_scales, w1, w2, offs, out):
         w1_bf = keep.tile([P, PACK * P * PACK], BF16, name="w1_bf", tag="w1_bf_then_words", align_bytes=64)
         dst = w1_bf[:].rearrange("p (t m j) -> p m j t", t=PACK, j=PACK)
         src = [raw[:].rearrange("p j (m t) -> p m j t", t=PACK) for raw in w1_raw]
-        for half in range(2):
-            for pair in range(2):
-                tiles = slice(2 * pair, 2 * pair + 2)
-                nc.scalar.activation(dst[:, :, 2 * half : 2 * half + 2, tiles], src[half][:, :, :, tiles], COPY)
+        low, high = slice(0, 2), slice(2, 4)
+        nc.scalar.activation(dst[:, :, low, low], src[0][:, :, :, low], COPY)
+        nc.scalar.activation(dst[:, :, low, high], src[0][:, :, :, high], COPY)
+        nc.scalar.activation(dst[:, :, high, low], src[1][:, :, :, low], COPY)
+        nc.scalar.activation(dst[:, :SPLIT, high, high], src[1][:, :SPLIT, :, high], COPY)
+        nc.vector.tensor_copy(dst[:, SPLIT:, high, high], src[1][:, SPLIT:, :, high])
         w1_codes = keep.tile([P, H], U32, name="w1_codes", align_bytes=64)
         w1_plane = keep.tile([P, H], U8, name="w1_plane", align_bytes=64)
-        for half in range(2):
-            cols = slice(half * H // 2, (half + 1) * H // 2)
+        for tile_pair in range(2):
+            cols = slice(tile_pair * H // 2, (tile_pair + 1) * H // 2)
             nc.vector.quantize_mx(
                 out=w1_codes[:, cols].bitcast(FP8X4),
                 scales=w1_plane[:, cols],
-                in_=w1_bf[:, half * H * PACK // 2 : (half + 1) * H * PACK // 2],
+                in_=w1_bf[:, tile_pair * H * PACK // 2 : (tile_pair + 1) * H * PACK // 2],
             )
         gather_words(pieces - 1, "w1_bf_then_words")
 

@@ -25,7 +25,7 @@ PIECE = 256
 CHUNK = 128
 HEAD = 768
 SPLIT = 64
-WARM_PASSES = 4
+WARM_WIDTHS = (PIECE, PIECE, 2 * PIECE, 2 * PIECE)
 
 
 def tile_picked_phmlp_relu_p_kernel(tc, x_words, x_scales, w1, w2, offs, out):
@@ -69,23 +69,23 @@ def tile_picked_phmlp_relu_p_kernel(tc, x_words, x_scales, w1, w2, offs, out):
 
         picked = []
 
-        def gather_words(g, tag):
-            words = keep.tile([P, PIECE], U32, name="picked_words%d" % g, tag=tag, align_bytes=64)
+        def gather_words(g, words):
             lists = offsets[:, g * PIECE // LIST_ROWS : (g + 1) * PIECE // LIST_ROWS]
-            nc.vector.tensor_copy(words[:], word_table[:].indirect(lists))
+            nc.vector.tensor_copy(words, word_table[:].indirect(lists))
             picked.append(words)
 
+        early_words = keep.tile([P, (pieces - 1) * PIECE], U32, name="early_words", align_bytes=64)
         for g in range(pieces - 1):
-            gather_words(g, "picked_words%d" % g)
+            gather_words(g, early_words[:, g * PIECE : (g + 1) * PIECE])
 
-        warm_bank = psum.tile([P, PIECE], F32, name="warm_bank", tag="bank")
-        for turn in range(WARM_PASSES):
+        warm_bank = psum.tile([P, 2 * PIECE], F32, name="warm_bank", tag="bank")
+        for width in WARM_WIDTHS:
             nc.tensor.matmul_mx(
-                out=warm_bank[:],
-                lhsT=picked[0][:, :P].bitcast(FP8X4),
+                out=warm_bank[:, :width],
+                lhsT=early_words[:, :P].bitcast(FP8X4),
                 lhsT_scale=picked_scales[:, :P],
-                rhs=picked[0][:].bitcast(FP8X4),
-                rhs_scale=picked_scales[:, :PIECE],
+                rhs=early_words[:, :width].bitcast(FP8X4),
+                rhs_scale=picked_scales[:, :width],
                 start=True,
                 stop=True,
             )
@@ -108,7 +108,8 @@ def tile_picked_phmlp_relu_p_kernel(tc, x_words, x_scales, w1, w2, offs, out):
                 scales=w1_plane[:, cols],
                 in_=w1_bf[:, tile_pair * H * PACK // 2 : (tile_pair + 1) * H * PACK // 2],
             )
-        gather_words(pieces - 1, "w1_bf_then_words")
+        last_words = keep.tile([P, PIECE], U32, name="last_words", tag="w1_bf_then_words", align_bytes=64)
+        gather_words(pieces - 1, last_words[:])
 
         w2_bf = keep.tile([P, N * PACK], BF16, name="w2_bf", align_bytes=64)
         nc.scalar.activation(

@@ -50,7 +50,7 @@ def tile_picked_phmlp_relu_p_kernel(tc, x_words, x_scales, w1, w2, offs, out):
         w1_rows = w1.rearrange("(p j) c -> p j c", j=PACK)
         w1_raw = []
         for row_pair in range(2):
-            raw = keep.tile([P, PACK // 2, H], F32, name="w1_raw%d" % row_pair)
+            raw = keep.tile([P, PACK // 2, H], F32, name="w1_raw%d" % row_pair, tag="w1_raw%d" % row_pair, align_bytes=64)
             nc.sync.dma_start(out=raw[:], in_=w1_rows[:, 2 * row_pair : 2 * row_pair + 2, :])
             w1_raw.append(raw)
             if row_pair == 0:
@@ -90,7 +90,7 @@ def tile_picked_phmlp_relu_p_kernel(tc, x_words, x_scales, w1, w2, offs, out):
                 stop=True,
             )
 
-        w1_bf = keep.tile([P, PACK * P * PACK], BF16, name="w1_bf", tag="w1_bf_then_words", align_bytes=64)
+        w1_bf = keep.tile([P, PACK * P * PACK], BF16, name="w1_bf", align_bytes=64)
         dst = w1_bf[:].rearrange("p (t m j) -> p m j t", t=PACK, j=PACK)
         src = [raw[:].rearrange("p j (m t) -> p m j t", t=PACK) for raw in w1_raw]
         low, high = slice(0, 2), slice(2, 4)
@@ -108,7 +108,7 @@ def tile_picked_phmlp_relu_p_kernel(tc, x_words, x_scales, w1, w2, offs, out):
                 scales=w1_plane[:, cols],
                 in_=w1_bf[:, tile_pair * H * PACK // 2 : (tile_pair + 1) * H * PACK // 2],
             )
-        last_words = keep.tile([P, PIECE], U32, name="last_words", tag="w1_bf_then_words", align_bytes=64)
+        last_words = keep.tile([P, PIECE], U32, name="last_words", tag="w1_raw1", align_bytes=64)
         gather_words(pieces - 1, last_words[:])
 
         w2_bf = keep.tile([P, N * PACK], BF16, name="w2_bf", align_bytes=64)
@@ -147,28 +147,27 @@ def tile_picked_phmlp_relu_p_kernel(tc, x_words, x_scales, w1, w2, offs, out):
         def quantize_hidden(g):
             nc.vector.quantize_mx(out=h_codes[g][:].bitcast(FP8X4), scales=h_plane[g][:], in_=h_bf[g][:])
 
-        out_view = out.rearrange("(u p) n -> p u n", p=P)
+        staged = [keep.tile([P, S], F32, name="staged%d" % u) for u in range(N // P)]
 
-        def second_layer(g, rows, on_vector):
-            bank = psum.tile([P, len(rows), PIECE], F32, name="o_bank", tag="bank")
-            for slot, u in enumerate(rows):
-                nc.tensor.matmul_mx(
-                    out=bank[:, slot, :],
-                    lhsT=w2_codes[:, u * P : (u + 1) * P].bitcast(FP8X4),
-                    lhsT_scale=w2_plane[:, u * P : (u + 1) * P],
-                    rhs=h_codes[g][:].bitcast(FP8X4),
-                    rhs_scale=h_plane[g][:],
-                    start=True,
-                    stop=True,
-                )
-            staged = keep.tile([P, len(rows), PIECE], F32, name="staged%d_%d" % (g, rows[0]))
-            if on_vector:
-                nc.vector.tensor_copy(staged[:], bank[:])
-            else:
-                nc.scalar.copy(staged[:], bank[:])
-            nc.sync.dma_start(
-                out=out_view[:, rows[0] : rows[-1] + 1, g * PIECE : (g + 1) * PIECE], in_=staged[:]
+        def second_layer(g, u, on_vector):
+            bank = psum.tile([P, PIECE], F32, name="o_bank", tag="bank")
+            nc.tensor.matmul_mx(
+                out=bank[:],
+                lhsT=w2_codes[:, u * P : (u + 1) * P].bitcast(FP8X4),
+                lhsT_scale=w2_plane[:, u * P : (u + 1) * P],
+                rhs=h_codes[g][:].bitcast(FP8X4),
+                rhs_scale=h_plane[g][:],
+                start=True,
+                stop=True,
             )
+            if on_vector:
+                nc.vector.tensor_copy(staged[u][:, g * PIECE : (g + 1) * PIECE], bank[:])
+            else:
+                nc.scalar.copy(staged[u][:, g * PIECE : (g + 1) * PIECE], bank[:])
+
+        def store(first, last, u):
+            cols = slice(first * PIECE, (last + 1) * PIECE)
+            nc.sync.dma_start(out=out[u * P : (u + 1) * P, cols], in_=staged[u][:, cols])
 
         hidden(0, False)
         nc.vector.quantize_mx(out=w2_codes[:].bitcast(FP8X4), scales=w2_plane[:], in_=w2_bf[:])
@@ -176,15 +175,26 @@ def tile_picked_phmlp_relu_p_kernel(tc, x_words, x_scales, w1, w2, offs, out):
         hidden(2, True)
         quantize_hidden(0)
         hidden(3, False)
-        quantize_hidden(1)
         hidden(4, False)
         hidden(5, True)
-        second_layer(0, [0, 1], False)
-        quantize_hidden(2)
-        hidden(7, False)
+        quantize_hidden(1)
         hidden(6, True)
-        second_layer(1, [0, 1], False)
+        second_layer(0, 0, False)
+        store(0, 0, 0)
+        hidden(7, False)
+        second_layer(0, 1, False)
+        store(0, 0, 1)
+        quantize_hidden(2)
         quantize_hidden(3)
-        second_layer(2, [0, 1], False)
-        second_layer(3, [0], True)
-        second_layer(3, [1], False)
+        second_layer(1, 0, True)
+        store(1, 1, 0)
+        second_layer(1, 1, False)
+        store(1, 1, 1)
+        second_layer(2, 0, True)
+        store(2, 2, 0)
+        second_layer(2, 1, False)
+        store(2, 2, 1)
+        second_layer(3, 0, True)
+        store(3, 3, 0)
+        second_layer(3, 1, False)
+        store(3, 3, 1)

@@ -24,7 +24,7 @@ BANKS = 8
 PIECE = 256
 CHUNK = 128
 HEAD = 768
-SPLIT = 64
+SPLIT = 48
 WARM_WIDTHS = (PIECE, PIECE, 2 * PIECE, 2 * PIECE)
 
 
@@ -50,7 +50,8 @@ def tile_picked_phmlp_relu_p_kernel(tc, x_words, x_scales, w1, w2, offs, out):
         w1_rows = w1.rearrange("(p j) c -> p j c", j=PACK)
         w1_raw = []
         for row_pair in range(2):
-            raw = keep.tile([P, PACK // 2, H], F32, name="w1_raw%d" % row_pair, tag="w1_raw%d" % row_pair, align_bytes=64)
+            tag = "w1_rows%d" % row_pair
+            raw = keep.tile([P, PACK // 2, H], F32, name=tag, tag=tag, align_bytes=64)
             nc.sync.dma_start(out=raw[:], in_=w1_rows[:, 2 * row_pair : 2 * row_pair + 2, :])
             w1_raw.append(raw)
             if row_pair == 0:
@@ -108,7 +109,7 @@ def tile_picked_phmlp_relu_p_kernel(tc, x_words, x_scales, w1, w2, offs, out):
                 scales=w1_plane[:, cols],
                 in_=w1_bf[:, tile_pair * H * PACK // 2 : (tile_pair + 1) * H * PACK // 2],
             )
-        last_words = keep.tile([P, PIECE], U32, name="last_words", tag="w1_raw1", align_bytes=64)
+        last_words = keep.tile([P, PIECE], U32, name="last_words", tag="w1_rows1", align_bytes=64)
         gather_words(pieces - 1, last_words[:])
 
         w2_bf = keep.tile([P, N * PACK], BF16, name="w2_bf", align_bytes=64)
@@ -144,30 +145,34 @@ def tile_picked_phmlp_relu_p_kernel(tc, x_words, x_scales, w1, w2, offs, out):
             else:
                 nc.scalar.activation(dst_h, src_h, RELU)
 
-        def quantize_hidden(g):
-            nc.vector.quantize_mx(out=h_codes[g][:].bitcast(FP8X4), scales=h_plane[g][:], in_=h_bf[g][:])
+        def quantize_hidden(g, lo=0, hi=PIECE):
+            nc.vector.quantize_mx(
+                out=h_codes[g][:, lo:hi].bitcast(FP8X4),
+                scales=h_plane[g][:, lo:hi],
+                in_=h_bf[g][:, lo * PACK : hi * PACK],
+            )
 
-        staged = [keep.tile([P, S], F32, name="staged%d" % u) for u in range(N // P)]
+        staged = [keep.tile([P, N // P, PIECE], F32, name="staged%d" % g) for g in range(pieces)]
+        out_view = out.rearrange("(u p) n -> p u n", p=P)
 
-        def second_layer(g, u, on_vector):
+        def second_layer(g, u, on_vector, lo=0, hi=PIECE):
             bank = psum.tile([P, PIECE], F32, name="o_bank", tag="bank")
             nc.tensor.matmul_mx(
-                out=bank[:],
+                out=bank[:, lo:hi],
                 lhsT=w2_codes[:, u * P : (u + 1) * P].bitcast(FP8X4),
                 lhsT_scale=w2_plane[:, u * P : (u + 1) * P],
-                rhs=h_codes[g][:].bitcast(FP8X4),
-                rhs_scale=h_plane[g][:],
+                rhs=h_codes[g][:, lo:hi].bitcast(FP8X4),
+                rhs_scale=h_plane[g][:, lo:hi],
                 start=True,
                 stop=True,
             )
             if on_vector:
-                nc.vector.tensor_copy(staged[u][:, g * PIECE : (g + 1) * PIECE], bank[:])
+                nc.vector.tensor_copy(staged[g][:, u, lo:hi], bank[:, lo:hi])
             else:
-                nc.scalar.copy(staged[u][:, g * PIECE : (g + 1) * PIECE], bank[:])
+                nc.scalar.copy(staged[g][:, u, lo:hi], bank[:, lo:hi])
 
-        def store(first, last, u):
-            cols = slice(first * PIECE, (last + 1) * PIECE)
-            nc.sync.dma_start(out=out[u * P : (u + 1) * P, cols], in_=staged[u][:, cols])
+        def store(g):
+            nc.sync.dma_start(out=out_view[:, :, g * PIECE : (g + 1) * PIECE], in_=staged[g][:])
 
         hidden(0, False)
         nc.vector.quantize_mx(out=w2_codes[:].bitcast(FP8X4), scales=w2_plane[:], in_=w2_bf[:])
@@ -180,21 +185,19 @@ def tile_picked_phmlp_relu_p_kernel(tc, x_words, x_scales, w1, w2, offs, out):
         quantize_hidden(1)
         hidden(6, True)
         second_layer(0, 0, False)
-        store(0, 0, 0)
-        hidden(7, False)
         second_layer(0, 1, False)
-        store(0, 0, 1)
+        store(0)
+        hidden(7, False)
         quantize_hidden(2)
-        quantize_hidden(3)
         second_layer(1, 0, True)
-        store(1, 1, 0)
         second_layer(1, 1, False)
-        store(1, 1, 1)
+        store(1)
+        for lo in (0, CHUNK):
+            quantize_hidden(3, lo, lo + CHUNK)
         second_layer(2, 0, True)
-        store(2, 2, 0)
         second_layer(2, 1, False)
-        store(2, 2, 1)
-        second_layer(3, 0, True)
-        store(3, 3, 0)
-        second_layer(3, 1, False)
-        store(3, 3, 1)
+        store(2)
+        for lo in (0, CHUNK):
+            second_layer(3, 0, True, lo, lo + CHUNK)
+            second_layer(3, 1, False, lo, lo + CHUNK)
+        store(3)

@@ -25,7 +25,8 @@ PIECE = 256
 CHUNK = 128
 HEAD = 768
 SPLIT = 48
-WARM_WIDTHS = (PIECE, PIECE, 2 * PIECE, 2 * PIECE)
+WARM_WIDTHS = (CHUNK, CHUNK, CHUNK, 2 * PIECE, 2 * PIECE)
+WARM_ROWS = 32
 
 
 def tile_picked_phmlp_relu_p_kernel(tc, x_words, x_scales, w1, w2, offs, out):
@@ -82,9 +83,9 @@ def tile_picked_phmlp_relu_p_kernel(tc, x_words, x_scales, w1, w2, offs, out):
         warm_bank = psum.tile([P, 2 * PIECE], F32, name="warm_bank", tag="bank")
         for width in WARM_WIDTHS:
             nc.tensor.matmul_mx(
-                out=warm_bank[:, :width],
-                lhsT=early_words[:, :P].bitcast(FP8X4),
-                lhsT_scale=picked_scales[:, :P],
+                out=warm_bank[:WARM_ROWS, :width],
+                lhsT=early_words[:, :WARM_ROWS].bitcast(FP8X4),
+                lhsT_scale=picked_scales[:, :WARM_ROWS],
                 rhs=early_words[:, :width].bitcast(FP8X4),
                 rhs_scale=picked_scales[:, :width],
                 start=True,

@@ -24,7 +24,7 @@ BANKS = 8
 PIECE = 256
 CHUNK = 128
 HEAD = 768
-SPLIT = 48
+SPLIT = 16
 WARM_WIDTHS = (CHUNK, CHUNK, CHUNK, 2 * PIECE, 2 * PIECE)
 WARM_ROWS = 32
 
@@ -36,9 +36,9 @@ def tile_picked_phmlp_relu_p_kernel(tc, x_words, x_scales, w1, w2, offs, out):
         keep = ctx.enter_context(tc.tile_pool(name="keep", bufs=1))
         psum = ctx.enter_context(tc.psum_pool(name="psum", bufs=BANKS))
 
-        word_table = keep.tile([P, T], U32, name="word_table", align_bytes=64)
-        word_rows = x_words[0].rearrange("p c r -> p (c r)").bitcast(I32)
-        nc.sync.dma_start(out=word_table[:, :HEAD].bitcast(I32), in_=word_rows[:, :HEAD])
+        w1_rows = w1.rearrange("(p j) c -> p j c", j=PACK)
+        w1_first = keep.tile([P, 1, H], F32, name="w1_first", tag="early", align_bytes=64)
+        nc.sync.dma_start(out=w1_first[:], in_=w1_rows[:, 0:1, :])
         offsets = keep.tile([P, S // LIST_ROWS], U16, name="offsets")
         nc.sync.dma_start(offsets[:], offs)
 
@@ -47,16 +47,11 @@ def tile_picked_phmlp_relu_p_kernel(tc, x_words, x_scales, w1, w2, offs, out):
         nc.sync.dma_start(out=scale_table[0:P:BLOCK_ROWS, :].bitcast(I32), in_=x_scales[0].bitcast(I32))
         x_plane = keep.tile([P, S], U8, name="x_plane", align_bytes=64)
         nc.vector.memset(x_plane[:].bitcast(I32), 0)
-
-        w1_rows = w1.rearrange("(p j) c -> p j c", j=PACK)
-        w1_raw = []
-        for row_pair in range(2):
-            tag = "w1_rows%d" % row_pair
-            raw = keep.tile([P, PACK // 2, H], F32, name=tag, tag=tag, align_bytes=64)
-            nc.sync.dma_start(out=raw[:], in_=w1_rows[:, 2 * row_pair : 2 * row_pair + 2, :])
-            w1_raw.append(raw)
-            if row_pair == 0:
-                nc.sync.dma_start(out=word_table[:, HEAD:].bitcast(I32), in_=word_rows[:, HEAD:])
+        word_table = keep.tile([P, T], U32, name="word_table", align_bytes=64)
+        word_rows = x_words[0].rearrange("p c r -> p (c r)").bitcast(I32)
+        nc.sync.dma_start(out=word_table[:].bitcast(I32), in_=word_rows)
+        w1_rest = keep.tile([P, PACK - 1, H], F32, name="w1_rest", tag="w1_rows1", align_bytes=64)
+        nc.sync.dma_start(out=w1_rest[:], in_=w1_rows[:, 1:, :])
 
         w2_raw = keep.tile([P, PACK, N], F32, name="w2_raw")
         nc.sync.dma_start(out=w2_raw[:], in_=w2.rearrange("(p j) n -> p j n", j=PACK))
@@ -69,6 +64,9 @@ def tile_picked_phmlp_relu_p_kernel(tc, x_words, x_scales, w1, w2, offs, out):
                 in_=picked_scales[BLOCK_ROWS * r : P : QUADRANT, :].bitcast(I32),
             )
 
+        w1_bf = keep.tile([P, PACK * P * PACK], BF16, name="w1_bf", align_bytes=64)
+        dst = w1_bf[:].rearrange("p (t m j) -> p m j t", t=PACK, j=PACK)
+        nc.scalar.activation(dst[:, :, 0:1, :], w1_first[:].rearrange("p j (m t) -> p m j t", t=PACK), COPY)
         picked = []
 
         def gather_words(g, words):
@@ -76,7 +74,7 @@ def tile_picked_phmlp_relu_p_kernel(tc, x_words, x_scales, w1, w2, offs, out):
             nc.vector.tensor_copy(words, word_table[:].indirect(lists))
             picked.append(words)
 
-        early_words = keep.tile([P, (pieces - 1) * PIECE], U32, name="early_words", align_bytes=64)
+        early_words = keep.tile([P, (pieces - 1) * PIECE], U32, name="early_words", tag="early", align_bytes=64)
         for g in range(pieces - 1):
             gather_words(g, early_words[:, g * PIECE : (g + 1) * PIECE])
 
@@ -92,15 +90,11 @@ def tile_picked_phmlp_relu_p_kernel(tc, x_words, x_scales, w1, w2, offs, out):
                 stop=True,
             )
 
-        w1_bf = keep.tile([P, PACK * P * PACK], BF16, name="w1_bf", align_bytes=64)
-        dst = w1_bf[:].rearrange("p (t m j) -> p m j t", t=PACK, j=PACK)
-        src = [raw[:].rearrange("p j (m t) -> p m j t", t=PACK) for raw in w1_raw]
+        rest = w1_rest[:].rearrange("p j (m t) -> p m j t", t=PACK)
         low, high = slice(0, 2), slice(2, 4)
-        nc.scalar.activation(dst[:, :, low, low], src[0][:, :, :, low], COPY)
-        nc.scalar.activation(dst[:, :, low, high], src[0][:, :, :, high], COPY)
-        nc.scalar.activation(dst[:, :, high, low], src[1][:, :, :, low], COPY)
-        nc.scalar.activation(dst[:, :SPLIT, high, high], src[1][:, :SPLIT, :, high], COPY)
-        nc.vector.tensor_copy(dst[:, SPLIT:, high, high], src[1][:, SPLIT:, :, high])
+        nc.scalar.activation(dst[:, :, 1:, low], rest[:, :, :, low], COPY)
+        nc.scalar.activation(dst[:, :SPLIT, 1:, high], rest[:, :SPLIT, :, high], COPY)
+        nc.vector.tensor_copy(dst[:, SPLIT:, 1:, high], rest[:, SPLIT:, :, high])
         w1_codes = keep.tile([P, H], U32, name="w1_codes", align_bytes=64)
         w1_plane = keep.tile([P, H], U8, name="w1_plane", align_bytes=64)
         for tile_pair in range(2):

@@ -24,7 +24,7 @@ BANKS = 8
 PIECE = 256
 CHUNK = 128
 HEAD = 768
-SPLIT = 16
+SPLIT = 24
 WARM_WIDTHS = (CHUNK, CHUNK, CHUNK, 2 * PIECE, 2 * PIECE)
 WARM_ROWS = 32
 
@@ -36,9 +36,9 @@ def tile_picked_phmlp_relu_p_kernel(tc, x_words, x_scales, w1, w2, offs, out):
         keep = ctx.enter_context(tc.tile_pool(name="keep", bufs=1))
         psum = ctx.enter_context(tc.psum_pool(name="psum", bufs=BANKS))
 
-        w1_rows = w1.rearrange("(p j) c -> p j c", j=PACK)
-        w1_first = keep.tile([P, 1, H], F32, name="w1_first", tag="early", align_bytes=64)
-        nc.sync.dma_start(out=w1_first[:], in_=w1_rows[:, 0:1, :])
+        w1_halves = w1.rearrange("(p j) (e c) -> p (j e) c", j=PACK, e=2)
+        w1_first = keep.tile([P, 3, H // 2], F32, name="w1_first", tag="early", align_bytes=64)
+        nc.sync.dma_start(out=w1_first[:], in_=w1_halves[:, :3, :])
         offsets = keep.tile([P, S // LIST_ROWS], U16, name="offsets")
         nc.sync.dma_start(offsets[:], offs)
 
@@ -50,8 +50,8 @@ def tile_picked_phmlp_relu_p_kernel(tc, x_words, x_scales, w1, w2, offs, out):
         word_table = keep.tile([P, T], U32, name="word_table", align_bytes=64)
         word_rows = x_words[0].rearrange("p c r -> p (c r)").bitcast(I32)
         nc.sync.dma_start(out=word_table[:].bitcast(I32), in_=word_rows)
-        w1_rest = keep.tile([P, PACK - 1, H], F32, name="w1_rest", tag="w1_rows1", align_bytes=64)
-        nc.sync.dma_start(out=w1_rest[:], in_=w1_rows[:, 1:, :])
+        w1_rest = keep.tile([P, 5, H // 2], F32, name="w1_rest", tag="w1_rows1", align_bytes=64)
+        nc.sync.dma_start(out=w1_rest[:], in_=w1_halves[:, 3:, :])
 
         w2_raw = keep.tile([P, PACK, N], F32, name="w2_raw")
         nc.sync.dma_start(out=w2_raw[:], in_=w2.rearrange("(p j) n -> p j n", j=PACK))
@@ -66,7 +66,12 @@ def tile_picked_phmlp_relu_p_kernel(tc, x_words, x_scales, w1, w2, offs, out):
 
         w1_bf = keep.tile([P, PACK * P * PACK], BF16, name="w1_bf", align_bytes=64)
         dst = w1_bf[:].rearrange("p (t m j) -> p m j t", t=PACK, j=PACK)
-        nc.scalar.activation(dst[:, :, 0:1, :], w1_first[:].rearrange("p j (m t) -> p m j t", t=PACK), COPY)
+        left, right = slice(0, P // 2), slice(P // 2, P)
+        low, high = slice(0, 2), slice(2, 4)
+        first = w1_first[:].rearrange("p h (m t) -> p m h t", t=PACK)
+        for tiles in (low, high):
+            nc.scalar.activation(dst[:, left, 0:2, tiles], first[:, :, 0:3:2, tiles], COPY)
+        nc.scalar.activation(dst[:, right, 0:1, :], first[:, :, 1:2, :], COPY)
         picked = []
 
         def gather_words(g, words):
@@ -90,11 +95,12 @@ def tile_picked_phmlp_relu_p_kernel(tc, x_words, x_scales, w1, w2, offs, out):
                 stop=True,
             )
 
-        rest = w1_rest[:].rearrange("p j (m t) -> p m j t", t=PACK)
-        low, high = slice(0, 2), slice(2, 4)
-        nc.scalar.activation(dst[:, :, 1:, low], rest[:, :, :, low], COPY)
-        nc.scalar.activation(dst[:, :SPLIT, 1:, high], rest[:, :SPLIT, :, high], COPY)
-        nc.vector.tensor_copy(dst[:, SPLIT:, 1:, high], rest[:, SPLIT:, :, high])
+        rest = w1_rest[:].rearrange("p h (m t) -> p m h t", t=PACK)
+        nc.scalar.activation(dst[:, left, 2:, low], rest[:, :, 1:5:2, low], COPY)
+        nc.scalar.activation(dst[:, right, 1:, low], rest[:, :, 0:5:2, low], COPY)
+        nc.scalar.activation(dst[:, :SPLIT, 2:, high], rest[:, :SPLIT, 1:5:2, high], COPY)
+        nc.vector.tensor_copy(dst[:, right, 1:, high], rest[:, :, 0:5:2, high])
+        nc.vector.tensor_copy(dst[:, SPLIT : P // 2, 2:, high], rest[:, SPLIT:, 1:5:2, high])
         w1_codes = keep.tile([P, H], U32, name="w1_codes", align_bytes=64)
         w1_plane = keep.tile([P, H], U8, name="w1_plane", align_bytes=64)
         for tile_pair in range(2):

@@ -23,8 +23,8 @@ QUADRANT = 32
 BANKS = 8
 PIECE = 256
 CHUNK = 128
-HEAD = 768
-SPLIT = 24
+LEAD = 3
+SPLIT = 48
 WARM_WIDTHS = (CHUNK, CHUNK, CHUNK, 2 * PIECE, 2 * PIECE)
 WARM_ROWS = 32
 
@@ -37,8 +37,8 @@ def tile_picked_phmlp_relu_p_kernel(tc, x_words, x_scales, w1, w2, offs, out):
         psum = ctx.enter_context(tc.psum_pool(name="psum", bufs=BANKS))
 
         w1_halves = w1.rearrange("(p j) (e c) -> p (j e) c", j=PACK, e=2)
-        w1_first = keep.tile([P, 3, H // 2], F32, name="w1_first", tag="early", align_bytes=64)
-        nc.sync.dma_start(out=w1_first[:], in_=w1_halves[:, :3, :])
+        w1_first = keep.tile([P, LEAD, H // 2], F32, name="w1_first", tag="early", align_bytes=64)
+        nc.sync.dma_start(out=w1_first[:], in_=w1_halves[:, :LEAD, :])
         offsets = keep.tile([P, S // LIST_ROWS], U16, name="offsets")
         nc.sync.dma_start(offsets[:], offs)
 
@@ -50,8 +50,8 @@ def tile_picked_phmlp_relu_p_kernel(tc, x_words, x_scales, w1, w2, offs, out):
         word_table = keep.tile([P, T], U32, name="word_table", align_bytes=64)
         word_rows = x_words[0].rearrange("p c r -> p (c r)").bitcast(I32)
         nc.sync.dma_start(out=word_table[:].bitcast(I32), in_=word_rows)
-        w1_rest = keep.tile([P, 5, H // 2], F32, name="w1_rest", tag="w1_rows1", align_bytes=64)
-        nc.sync.dma_start(out=w1_rest[:], in_=w1_halves[:, 3:, :])
+        w1_rest = keep.tile([P, 2 * PACK - LEAD, H // 2], F32, name="w1_rest", tag="late", align_bytes=64)
+        nc.sync.dma_start(out=w1_rest[:], in_=w1_halves[:, LEAD:, :])
 
         w2_raw = keep.tile([P, PACK, N], F32, name="w2_raw")
         nc.sync.dma_start(out=w2_raw[:], in_=w2.rearrange("(p j) n -> p j n", j=PACK))
@@ -67,21 +67,18 @@ def tile_picked_phmlp_relu_p_kernel(tc, x_words, x_scales, w1, w2, offs, out):
         w1_bf = keep.tile([P, PACK * P * PACK], BF16, name="w1_bf", align_bytes=64)
         dst = w1_bf[:].rearrange("p (t m j) -> p m j t", t=PACK, j=PACK)
         left, right = slice(0, P // 2), slice(P // 2, P)
-        low, high = slice(0, 2), slice(2, 4)
+        low_tiles, high_tiles = slice(0, 2), slice(2, 4)
         first = w1_first[:].rearrange("p h (m t) -> p m h t", t=PACK)
-        for tiles in (low, high):
-            nc.scalar.activation(dst[:, left, 0:2, tiles], first[:, :, 0:3:2, tiles], COPY)
+        for tiles in (low_tiles, high_tiles):
+            nc.scalar.activation(dst[:, left, 0:2, tiles], first[:, :, 0:LEAD:2, tiles], COPY)
         nc.scalar.activation(dst[:, right, 0:1, :], first[:, :, 1:2, :], COPY)
-        picked = []
 
-        def gather_words(g, words):
-            lists = offsets[:, g * PIECE // LIST_ROWS : (g + 1) * PIECE // LIST_ROWS]
-            nc.vector.tensor_copy(words, word_table[:].indirect(lists))
-            picked.append(words)
+        def gather_words(words, lo, hi):
+            nc.vector.tensor_copy(words, word_table[:].indirect(offsets[:, lo // LIST_ROWS : hi // LIST_ROWS]))
 
-        early_words = keep.tile([P, (pieces - 1) * PIECE], U32, name="early_words", tag="early", align_bytes=64)
-        for g in range(pieces - 1):
-            gather_words(g, early_words[:, g * PIECE : (g + 1) * PIECE])
+        early_words = keep.tile([P, 2 * PIECE], U32, name="early_words", tag="early", align_bytes=64)
+        for lo in (0, PIECE):
+            gather_words(early_words[:, lo : lo + PIECE], lo, lo + PIECE)
 
         warm_bank = psum.tile([P, 2 * PIECE], F32, name="warm_bank", tag="bank")
         for width in WARM_WIDTHS:
@@ -96,22 +93,24 @@ def tile_picked_phmlp_relu_p_kernel(tc, x_words, x_scales, w1, w2, offs, out):
             )
 
         rest = w1_rest[:].rearrange("p h (m t) -> p m h t", t=PACK)
-        nc.scalar.activation(dst[:, left, 2:, low], rest[:, :, 1:5:2, low], COPY)
-        nc.scalar.activation(dst[:, right, 1:, low], rest[:, :, 0:5:2, low], COPY)
-        nc.scalar.activation(dst[:, :SPLIT, 2:, high], rest[:, :SPLIT, 1:5:2, high], COPY)
-        nc.vector.tensor_copy(dst[:, right, 1:, high], rest[:, :, 0:5:2, high])
-        nc.vector.tensor_copy(dst[:, SPLIT : P // 2, 2:, high], rest[:, SPLIT:, 1:5:2, high])
+        rest_left, rest_right = rest[:, :, 1:4:2, :], rest[:, :, 0:5:2, :]
+        nc.scalar.activation(dst[:, left, 2:, low_tiles], rest_left[:, :, :, low_tiles], COPY)
+        nc.scalar.activation(dst[:, P // 2 : P // 2 + SPLIT, 1:, low_tiles], rest_right[:, :SPLIT, :, low_tiles], COPY)
+        nc.vector.tensor_copy(dst[:, left, 2:, high_tiles], rest_left[:, :, :, high_tiles])
+        nc.vector.tensor_copy(dst[:, right, 1:, high_tiles], rest_right[:, :, :, high_tiles])
+        nc.vector.tensor_copy(dst[:, P // 2 + SPLIT :, 1:, low_tiles], rest_right[:, SPLIT:, :, low_tiles])
         w1_codes = keep.tile([P, H], U32, name="w1_codes", align_bytes=64)
         w1_plane = keep.tile([P, H], U8, name="w1_plane", align_bytes=64)
-        for tile_pair in range(2):
+        for tile_pair in (1, 0):
             cols = slice(tile_pair * H // 2, (tile_pair + 1) * H // 2)
             nc.vector.quantize_mx(
                 out=w1_codes[:, cols].bitcast(FP8X4),
                 scales=w1_plane[:, cols],
                 in_=w1_bf[:, tile_pair * H * PACK // 2 : (tile_pair + 1) * H * PACK // 2],
             )
-        last_words = keep.tile([P, PIECE], U32, name="last_words", tag="w1_rows1", align_bytes=64)
-        gather_words(pieces - 1, last_words[:])
+        last_words = keep.tile([P, 2 * PIECE], U32, name="last_words", tag="late", align_bytes=64)
+        gather_words(last_words[:], 2 * PIECE, S)
+        picked = [words[:, lo : lo + PIECE] for words in (early_words, last_words) for lo in (0, PIECE)]
 
         w2_bf = keep.tile([P, N * PACK], BF16, name="w2_bf", align_bytes=64)
         nc.scalar.activation(
@@ -129,7 +128,7 @@ def tile_picked_phmlp_relu_p_kernel(tc, x_words, x_scales, w1, w2, offs, out):
         def hidden(c, on_vector):
             g, half = divmod(c, PIECE // CHUNK)
             bank = psum.tile([P, PACK, CHUNK], F32, name="h_bank", tag="bank")
-            for t in range(PACK):
+            for t in (2, 3, 0, 1):
                 nc.tensor.matmul_mx(
                     out=bank[:, t, :],
                     lhsT=w1_codes[:, t * P : (t + 1) * P].bitcast(FP8X4),

@@ -23,7 +23,8 @@ QUADRANT = 32
 BANKS = 8
 PIECE = 256
 CHUNK = 128
-LEAD = 3
+LEAD = 2
+EARLY = LEAD + 1
 SPLIT = 48
 WARM_WIDTHS = (CHUNK, CHUNK, CHUNK, 2 * PIECE, 2 * PIECE)
 WARM_ROWS = 32
@@ -43,15 +44,18 @@ def tile_picked_phmlp_relu_p_kernel(tc, x_words, x_scales, w1, w2, offs, out):
         nc.sync.dma_start(offsets[:], offs)
 
         scale_table = keep.tile([P, T], U8, name="scale_table", align_bytes=64)
-        nc.vector.memset(scale_table[:].bitcast(I32), 0)
+        nc.gpsimd.memset(scale_table[:, : T // 2].bitcast(I32), 0)
+        nc.vector.memset(scale_table[:, T // 2 :].bitcast(I32), 0)
         nc.sync.dma_start(out=scale_table[0:P:BLOCK_ROWS, :].bitcast(I32), in_=x_scales[0].bitcast(I32))
+        w1_second = keep.tile([P, H // 2], F32, name="w1_second", align_bytes=64)
+        nc.sync.dma_start(out=w1_second[:], in_=w1_halves[:, LEAD, :])
         x_plane = keep.tile([P, S], U8, name="x_plane", align_bytes=64)
         nc.vector.memset(x_plane[:].bitcast(I32), 0)
         word_table = keep.tile([P, T], U32, name="word_table", align_bytes=64)
         word_rows = x_words[0].rearrange("p c r -> p (c r)").bitcast(I32)
         nc.sync.dma_start(out=word_table[:].bitcast(I32), in_=word_rows)
-        w1_rest = keep.tile([P, 2 * PACK - LEAD, H // 2], F32, name="w1_rest", tag="late", align_bytes=64)
-        nc.sync.dma_start(out=w1_rest[:], in_=w1_halves[:, LEAD:, :])
+        w1_rest = keep.tile([P, 2 * PACK - EARLY, H // 2], F32, name="w1_rest", tag="late", align_bytes=64)
+        nc.sync.dma_start(out=w1_rest[:], in_=w1_halves[:, EARLY:, :])
 
         w2_raw = keep.tile([P, PACK, N], F32, name="w2_raw")
         nc.sync.dma_start(out=w2_raw[:], in_=w2.rearrange("(p j) n -> p j n", j=PACK))
@@ -68,10 +72,9 @@ def tile_picked_phmlp_relu_p_kernel(tc, x_words, x_scales, w1, w2, offs, out):
         dst = w1_bf[:].rearrange("p (t m j) -> p m j t", t=PACK, j=PACK)
         left, right = slice(0, P // 2), slice(P // 2, P)
         low_tiles, high_tiles = slice(0, 2), slice(2, 4)
-        first = w1_first[:].rearrange("p h (m t) -> p m h t", t=PACK)
-        for tiles in (low_tiles, high_tiles):
-            nc.scalar.activation(dst[:, left, 0:2, tiles], first[:, :, 0:LEAD:2, tiles], COPY)
-        nc.scalar.activation(dst[:, right, 0:1, :], first[:, :, 1:2, :], COPY)
+        first = w1_first[:].rearrange("p h (m t) -> p (h m) t", t=PACK)
+        nc.scalar.activation(dst[:, :, 0, :], first, COPY)
+        nc.scalar.activation(dst[:, left, 1, :], w1_second[:].rearrange("p (m t) -> p m t", t=PACK), COPY)
 
         def gather_words(words, lo, hi):
             nc.vector.tensor_copy(words, word_table[:].indirect(offsets[:, lo // LIST_ROWS : hi // LIST_ROWS]))

@@ -23,9 +23,7 @@ QUADRANT = 32
 BANKS = 8
 PIECE = 256
 CHUNK = 128
-LEAD = 2
-EARLY = LEAD + 1
-SPLIT = 48
+SPLIT = 100
 WARM_WIDTHS = (CHUNK, CHUNK, CHUNK, 2 * PIECE, 2 * PIECE)
 WARM_ROWS = 32
 
@@ -37,9 +35,9 @@ def tile_picked_phmlp_relu_p_kernel(tc, x_words, x_scales, w1, w2, offs, out):
         keep = ctx.enter_context(tc.tile_pool(name="keep", bufs=1))
         psum = ctx.enter_context(tc.psum_pool(name="psum", bufs=BANKS))
 
-        w1_halves = w1.rearrange("(p j) (e c) -> p (j e) c", j=PACK, e=2)
-        w1_first = keep.tile([P, LEAD, H // 2], F32, name="w1_first", tag="early", align_bytes=64)
-        nc.sync.dma_start(out=w1_first[:], in_=w1_halves[:, :LEAD, :])
+        w1_rows = w1.rearrange("(p j) c -> p j c", j=PACK)
+        w1_first = keep.tile([P, H], F32, name="w1_first", tag="early", align_bytes=64)
+        nc.sync.dma_start(out=w1_first[:], in_=w1_rows[:, 0, :])
         offsets = keep.tile([P, S // LIST_ROWS], U16, name="offsets")
         nc.sync.dma_start(offsets[:], offs)
 
@@ -47,15 +45,13 @@ def tile_picked_phmlp_relu_p_kernel(tc, x_words, x_scales, w1, w2, offs, out):
         nc.gpsimd.memset(scale_table[:, : T // 2].bitcast(I32), 0)
         nc.vector.memset(scale_table[:, T // 2 :].bitcast(I32), 0)
         nc.sync.dma_start(out=scale_table[0:P:BLOCK_ROWS, :].bitcast(I32), in_=x_scales[0].bitcast(I32))
-        w1_second = keep.tile([P, H // 2], F32, name="w1_second", align_bytes=64)
-        nc.sync.dma_start(out=w1_second[:], in_=w1_halves[:, LEAD, :])
         x_plane = keep.tile([P, S], U8, name="x_plane", align_bytes=64)
         nc.vector.memset(x_plane[:].bitcast(I32), 0)
         word_table = keep.tile([P, T], U32, name="word_table", align_bytes=64)
         word_rows = x_words[0].rearrange("p c r -> p (c r)").bitcast(I32)
         nc.sync.dma_start(out=word_table[:].bitcast(I32), in_=word_rows)
-        w1_rest = keep.tile([P, 2 * PACK - EARLY, H // 2], F32, name="w1_rest", tag="late", align_bytes=64)
-        nc.sync.dma_start(out=w1_rest[:], in_=w1_halves[:, EARLY:, :])
+        w1_rest = keep.tile([P, PACK - 1, H], F32, name="w1_rest", tag="late", align_bytes=64)
+        nc.sync.dma_start(out=w1_rest[:], in_=w1_rows[:, 1:, :])
 
         w2_raw = keep.tile([P, PACK, N], F32, name="w2_raw")
         nc.sync.dma_start(out=w2_raw[:], in_=w2.rearrange("(p j) n -> p j n", j=PACK))
@@ -68,13 +64,10 @@ def tile_picked_phmlp_relu_p_kernel(tc, x_words, x_scales, w1, w2, offs, out):
                 in_=picked_scales[BLOCK_ROWS * r : P : QUADRANT, :].bitcast(I32),
             )
 
-        w1_bf = keep.tile([P, PACK * P * PACK], BF16, name="w1_bf", align_bytes=64)
+        w1_bf = keep.tile([P, PACK * P * PACK], BF16, name="w1_bf", tag="rounded", align_bytes=64)
         dst = w1_bf[:].rearrange("p (t m j) -> p m j t", t=PACK, j=PACK)
-        left, right = slice(0, P // 2), slice(P // 2, P)
         low_tiles, high_tiles = slice(0, 2), slice(2, 4)
-        first = w1_first[:].rearrange("p h (m t) -> p (h m) t", t=PACK)
-        nc.scalar.activation(dst[:, :, 0, :], first, COPY)
-        nc.scalar.activation(dst[:, left, 1, :], w1_second[:].rearrange("p (m t) -> p m t", t=PACK), COPY)
+        nc.scalar.activation(dst[:, :, 0, :], w1_first[:].rearrange("p (m t) -> p m t", t=PACK), COPY)
 
         def gather_words(words, lo, hi):
             nc.vector.tensor_copy(words, word_table[:].indirect(offsets[:, lo // LIST_ROWS : hi // LIST_ROWS]))
@@ -95,13 +88,10 @@ def tile_picked_phmlp_relu_p_kernel(tc, x_words, x_scales, w1, w2, offs, out):
                 stop=True,
             )
 
-        rest = w1_rest[:].rearrange("p h (m t) -> p m h t", t=PACK)
-        rest_left, rest_right = rest[:, :, 1:4:2, :], rest[:, :, 0:5:2, :]
-        nc.scalar.activation(dst[:, left, 2:, low_tiles], rest_left[:, :, :, low_tiles], COPY)
-        nc.scalar.activation(dst[:, P // 2 : P // 2 + SPLIT, 1:, low_tiles], rest_right[:, :SPLIT, :, low_tiles], COPY)
-        nc.vector.tensor_copy(dst[:, left, 2:, high_tiles], rest_left[:, :, :, high_tiles])
-        nc.vector.tensor_copy(dst[:, right, 1:, high_tiles], rest_right[:, :, :, high_tiles])
-        nc.vector.tensor_copy(dst[:, P // 2 + SPLIT :, 1:, low_tiles], rest_right[:, SPLIT:, :, low_tiles])
+        rest = w1_rest[:].rearrange("p j (m t) -> p m j t", t=PACK)
+        nc.scalar.activation(dst[:, :SPLIT, 1:, low_tiles], rest[:, :SPLIT, :, low_tiles], COPY)
+        nc.vector.tensor_copy(dst[:, :, 1:, high_tiles], rest[:, :, :, high_tiles])
+        nc.vector.tensor_copy(dst[:, SPLIT:, 1:, low_tiles], rest[:, SPLIT:, :, low_tiles])
         w1_codes = keep.tile([P, H], U32, name="w1_codes", align_bytes=64)
         w1_plane = keep.tile([P, H], U8, name="w1_plane", align_bytes=64)
         for tile_pair in (1, 0):
@@ -115,12 +105,15 @@ def tile_picked_phmlp_relu_p_kernel(tc, x_words, x_scales, w1, w2, offs, out):
         gather_words(last_words[:], 2 * PIECE, S)
         picked = [words[:, lo : lo + PIECE] for words in (early_words, last_words) for lo in (0, PIECE)]
 
-        w2_bf = keep.tile([P, N * PACK], BF16, name="w2_bf", align_bytes=64)
+        w2_bf = [
+            keep.tile([P, P * PACK], BF16, name="w2_bf", tag=tag, align_bytes=64) for tag in ("w2_low", "rounded")
+        ]
         nc.scalar.activation(
-            w2_bf[:].rearrange("p (c i j) -> p c j i", i=4, j=PACK),
-            w2_raw[:].rearrange("p j (c i) -> p c j i", i=4),
+            w2_bf[0][:].rearrange("p (c i j) -> p c j i", i=4, j=PACK),
+            w2_raw[:, :, :P].rearrange("p j (c i) -> p c j i", i=4),
             COPY,
         )
+        nc.gpsimd.tensor_copy(w2_bf[1][:].rearrange("p (n j) -> p n j", j=PACK), w2_raw[:, :, P:].rearrange("p j n -> p n j"))
         w2_codes = keep.tile([P, N], U32, name="w2_codes", align_bytes=64)
         w2_plane = keep.tile([P, N], U8, name="w2_plane", align_bytes=64)
 
@@ -178,7 +171,9 @@ def tile_picked_phmlp_relu_p_kernel(tc, x_words, x_scales, w1, w2, offs, out):
             nc.sync.dma_start(out=out_view[:, :, g * PIECE : (g + 1) * PIECE], in_=staged[g][:])
 
         hidden(0, False)
-        nc.vector.quantize_mx(out=w2_codes[:].bitcast(FP8X4), scales=w2_plane[:], in_=w2_bf[:])
+        for u in range(N // P):
+            cols = slice(u * P, (u + 1) * P)
+            nc.vector.quantize_mx(out=w2_codes[:, cols].bitcast(FP8X4), scales=w2_plane[:, cols], in_=w2_bf[u][:])
         hidden(1, False)
         hidden(2, True)
         quantize_hidden(0)

from contextlib import ExitStack

import concourse.mybir as mybir

K, T, S, H, N = 512, 2048, 1024, 512, 256
FLOPS = 2 * K * H * S + 2 * H * N * S

F32 = mybir.dt.float32
BF16 = mybir.dt.bfloat16
I32 = mybir.dt.int32
U32 = mybir.dt.uint32
U16 = mybir.dt.uint16
U8 = mybir.dt.uint8
FP8X4 = mybir.dt.float8_e4m3fn_x4
RELU = mybir.ActivationFunctionType.Relu
COPY = mybir.ActivationFunctionType.Copy

P = 128
PACK = 4
LIST_ROWS = 16
BLOCK_ROWS = 8
QUADRANT = 32
BANKS = 8
PIECE = 256
CHUNK = 128
SPLIT = 100
WARM_WIDTHS = (CHUNK, CHUNK, CHUNK, 2 * PIECE, 2 * PIECE)
WARM_ROWS = 32


def tile_picked_phmlp_relu_p_kernel(tc, x_words, x_scales, w1, w2, offs, out):
    nc = tc.nc
    pieces = S // PIECE
    with ExitStack() as ctx:
        keep = ctx.enter_context(tc.tile_pool(name="keep", bufs=1))
        psum = ctx.enter_context(tc.psum_pool(name="psum", bufs=BANKS))

        w1_rows = w1.rearrange("(p j) c -> p j c", j=PACK)
        w1_first = keep.tile([P, H], F32, name="w1_first", tag="early", align_bytes=64)
        nc.sync.dma_start(out=w1_first[:], in_=w1_rows[:, 0, :])
        offsets = keep.tile([P, S // LIST_ROWS], U16, name="offsets")
        nc.sync.dma_start(offsets[:], offs)

        scale_table = keep.tile([P, T], U8, name="scale_table", align_bytes=64)
        nc.gpsimd.memset(scale_table[:, : T // 2].bitcast(I32), 0)
        nc.vector.memset(scale_table[:, T // 2 :].bitcast(I32), 0)
        nc.sync.dma_start(out=scale_table[0:P:BLOCK_ROWS, :].bitcast(I32), in_=x_scales[0].bitcast(I32))
        x_plane = keep.tile([P, S], U8, name="x_plane", align_bytes=64)
        nc.vector.memset(x_plane[:].bitcast(I32), 0)
        word_table = keep.tile([P, T], U32, name="word_table", align_bytes=64)
        word_rows = x_words[0].rearrange("p c r -> p (c r)").bitcast(I32)
        nc.sync.dma_start(out=word_table[:].bitcast(I32), in_=word_rows)
        w1_rest = keep.tile([P, PACK - 1, H], F32, name="w1_rest", tag="late", align_bytes=64)
        nc.sync.dma_start(out=w1_rest[:], in_=w1_rows[:, 1:, :])

        w2_raw = keep.tile([P, PACK, N], F32, name="w2_raw")
        nc.sync.dma_start(out=w2_raw[:], in_=w2.rearrange("(p j) n -> p j n", j=PACK))

        picked_scales = keep.tile([P, S], U8, name="picked_scales", align_bytes=64)
        nc.vector.tensor_copy(picked_scales[:], scale_table[:].indirect(offsets[:]))
        for r in range(QUADRANT // BLOCK_ROWS):
            nc.sync.dma_start(
                out=x_plane[r:P:QUADRANT, :].bitcast(I32),
                in_=picked_scales[BLOCK_ROWS * r : P : QUADRANT, :].bitcast(I32),
            )

        w1_bf = keep.tile([P, PACK * P * PACK], BF16, name="w1_bf", tag="rounded", align_bytes=64)
        dst = w1_bf[:].rearrange("p (t m j) -> p m j t", t=PACK, j=PACK)
        low_tiles, high_tiles = slice(0, 2), slice(2, 4)
        nc.scalar.activation(dst[:, :, 0, :], w1_first[:].rearrange("p (m t) -> p m t", t=PACK), COPY)

        def gather_words(words, lo, hi):
            nc.vector.tensor_copy(words, word_table[:].indirect(offsets[:, lo // LIST_ROWS : hi // LIST_ROWS]))

        early_words = keep.tile([P, 2 * PIECE], U32, name="early_words", tag="early", align_bytes=64)
        for lo in (0, PIECE):
            gather_words(early_words[:, lo : lo + PIECE], lo, lo + PIECE)

        warm_bank = psum.tile([P, 2 * PIECE], F32, name="warm_bank", tag="bank")
        for width in WARM_WIDTHS:
            nc.tensor.matmul_mx(
                out=warm_bank[:WARM_ROWS, :width],
                lhsT=early_words[:, :WARM_ROWS].bitcast(FP8X4),
                lhsT_scale=picked_scales[:, :WARM_ROWS],
                rhs=early_words[:, :width].bitcast(FP8X4),
                rhs_scale=picked_scales[:, :width],
                start=True,
                stop=True,
            )

        rest = w1_rest[:].rearrange("p j (m t) -> p m j t", t=PACK)
        nc.scalar.activation(dst[:, :SPLIT, 1:, low_tiles], rest[:, :SPLIT, :, low_tiles], COPY)
        nc.vector.tensor_copy(dst[:, :, 1:, high_tiles], rest[:, :, :, high_tiles])
        nc.vector.tensor_copy(dst[:, SPLIT:, 1:, low_tiles], rest[:, SPLIT:, :, low_tiles])
        w1_codes = keep.tile([P, H], U32, name="w1_codes", align_bytes=64)
        w1_plane = keep.tile([P, H], U8, name="w1_plane", align_bytes=64)
        for tile_pair in (1, 0):
            cols = slice(tile_pair * H // 2, (tile_pair + 1) * H // 2)
            nc.vector.quantize_mx(
                out=w1_codes[:, cols].bitcast(FP8X4),
                scales=w1_plane[:, cols],
                in_=w1_bf[:, tile_pair * H * PACK // 2 : (tile_pair + 1) * H * PACK // 2],
            )
        last_words = keep.tile([P, 2 * PIECE], U32, name="last_words", tag="late", align_bytes=64)
        gather_words(last_words[:], 2 * PIECE, S)
        picked = [words[:, lo : lo + PIECE] for words in (early_words, last_words) for lo in (0, PIECE)]

        w2_bf = [
            keep.tile([P, P * PACK], BF16, name="w2_bf", tag=tag, align_bytes=64) for tag in ("w2_low", "rounded")
        ]
        nc.scalar.activation(
            w2_bf[0][:].rearrange("p (c i j) -> p c j i", i=4, j=PACK),
            w2_raw[:, :, :P].rearrange("p j (c i) -> p c j i", i=4),
            COPY,
        )
        nc.gpsimd.tensor_copy(w2_bf[1][:].rearrange("p (n j) -> p n j", j=PACK), w2_raw[:, :, P:].rearrange("p j n -> p n j"))
        w2_codes = keep.tile([P, N], U32, name="w2_codes", align_bytes=64)
        w2_plane = keep.tile([P, N], U8, name="w2_plane", align_bytes=64)

        h_bf = [keep.tile([P, PIECE * PACK], BF16, name="h_bf%d" % g, align_bytes=64) for g in range(pieces)]
        h_codes = [keep.tile([P, PIECE], U32, name="h_codes%d" % g, align_bytes=64) for g in range(pieces)]
        h_plane = [keep.tile([P, PIECE], U8, name="h_plane%d" % g, align_bytes=64) for g in range(pieces)]

        def hidden(c, on_vector):
            g, half = divmod(c, PIECE // CHUNK)
            bank = psum.tile([P, PACK, CHUNK], F32, name="h_bank", tag="bank")
            for t in (2, 3, 0, 1):
                nc.tensor.matmul_mx(
                    out=bank[:, t, :],
                    lhsT=w1_codes[:, t * P : (t + 1) * P].bitcast(FP8X4),
                    lhsT_scale=w1_plane[:, t * P : (t + 1) * P],
                    rhs=picked[g][:, half * CHUNK : (half + 1) * CHUNK].bitcast(FP8X4),
                    rhs_scale=x_plane[:, c * CHUNK : (c + 1) * CHUNK],
                    start=True,
                    stop=True,
                )
            dst_h = h_bf[g][:, half * CHUNK * PACK : (half + 1) * CHUNK * PACK].rearrange("p (n t) -> p n t", t=PACK)
            src_h = bank[:].rearrange("p t n -> p n t")
            if on_vector:
                nc.vector.tensor_scalar_max(dst_h, src_h, 0.0)
            else:
                nc.scalar.activation(dst_h, src_h, RELU)

        def quantize_hidden(g, lo=0, hi=PIECE):
            nc.vector.quantize_mx(
                out=h_codes[g][:, lo:hi].bitcast(FP8X4),
                scales=h_plane[g][:, lo:hi],
                in_=h_bf[g][:, lo * PACK : hi * PACK],
            )

        staged = [keep.tile([P, N // P, PIECE], F32, name="staged%d" % g) for g in range(pieces)]
        out_view = out.rearrange("(u p) n -> p u n", p=P)

        def second_layer(g, u, on_vector, lo=0, hi=PIECE):
            bank = psum.tile([P, PIECE], F32, name="o_bank", tag="bank")
            nc.tensor.matmul_mx(
                out=bank[:, lo:hi],
                lhsT=w2_codes[:, u * P : (u + 1) * P].bitcast(FP8X4),
                lhsT_scale=w2_plane[:, u * P : (u + 1) * P],
                rhs=h_codes[g][:, lo:hi].bitcast(FP8X4),
                rhs_scale=h_plane[g][:, lo:hi],
                start=True,
                stop=True,
            )
            if on_vector:
                nc.vector.tensor_copy(staged[g][:, u, lo:hi], bank[:, lo:hi])
            else:
                nc.scalar.copy(staged[g][:, u, lo:hi], bank[:, lo:hi])

        def store(g):
            nc.sync.dma_start(out=out_view[:, :, g * PIECE : (g + 1) * PIECE], in_=staged[g][:])

        hidden(0, False)
        for u in range(N // P):
            cols = slice(u * P, (u + 1) * P)
            nc.vector.quantize_mx(out=w2_codes[:, cols].bitcast(FP8X4), scales=w2_plane[:, cols], in_=w2_bf[u][:])
        hidden(1, False)
        hidden(2, True)
        quantize_hidden(0)
        hidden(3, False)
        hidden(4, False)
        hidden(5, True)
        quantize_hidden(1)
        hidden(6, True)
        second_layer(0, 0, False)
        second_layer(0, 1, False)
        store(0)
        hidden(7, False)
        quantize_hidden(2)
        second_layer(1, 0, True)
        second_layer(1, 1, False)
        store(1)
        for lo in (0, CHUNK):
            quantize_hidden(3, lo, lo + CHUNK)
        second_layer(2, 0, True)
        second_layer(2, 1, False)
        store(2)
        for lo in (0, CHUNK):
            second_layer(3, 0, True, lo, lo + CHUNK)
            second_layer(3, 1, False, lo, lo + CHUNK)
        store(3)
